import numpy as np
import ml_dtypes


def mxq(x, axis, fmt="e4m3"):
    dtype, down = {"e4m3": (ml_dtypes.float8_e4m3fn, 7), "e5m2": (ml_dtypes.float8_e5m2, 14)}[fmt]
    v = np.moveaxis(np.asarray(x, np.float32).astype(ml_dtypes.bfloat16).astype(np.float64), axis, -1)
    blocks = v.reshape(v.shape[:-1] + (-1, 32))
    amax = np.abs(blocks).max(-1, keepdims=True)
    byte = np.maximum(np.where(amax > 0, np.frexp(amax)[1] - 1 + 127, 0) - down, 1)
    scale = np.exp2(byte - 127.0)
    codes = (blocks / scale).astype(np.float32).astype(dtype).astype(np.float64)
    return np.moveaxis((codes * scale).reshape(v.shape), -1, axis)


WIDE = False


def mx_kscale(k):
    if not WIDE:
        return np.ones(k)
    levels = np.array([10, -10, 5, -5, 0])
    if k % 512:
        return np.exp2(np.random.permutation(np.resize(levels, k // 32))).repeat(32)
    a = np.empty((k // 512, 16))
    for p in range(k // 512):
        a[p, :8] = np.random.permutation(np.resize(levels, 8))
        for g in range(8):
            far = levels[np.abs(levels - a[p, g]) >= 10]
            a[p, g + 8] = far[np.random.randint(len(far))]
    return np.exp2(a.ravel()).repeat(32)


def f64(x):
    return np.asarray(x).astype(np.float64)


def striped8(idx):
    return np.asarray(idx).reshape(8, -1, 16).transpose(0, 2, 1).reshape(128, -1).astype(np.uint16)


def unstriped8(offs):
    return offs.reshape(8, 16, -1).transpose(0, 2, 1).reshape(8, -1).astype(np.int64)


def pick8(x, idx, run):
    r = np.arange(len(x))
    return x[r[:, None], idx[r % (8 * run) // run]]


E2M1 = np.array([0.0, 0.5, 1.0, 1.5, 2.0, 3.0, 4.0, 6.0, -0.0, -0.5, -1.0, -1.5, -2.0, -3.0, -4.0, -6.0])


def pack_weight(w, fmt):
    k, n = w.shape
    w = f64(np.asarray(w, np.float32).astype(ml_dtypes.bfloat16)).reshape(k // 32, 32, n)
    amax = np.abs(w).max(1)
    if fmt == "e4m3":
        byte = np.frexp(amax)[1] - 1 + 127 - 7
    else:
        mant, ex = np.frexp(amax / 6.0)
        byte = np.where(mant > 0.5, ex, ex - 1) + 127
    byte = np.clip(np.where(amax > 0, byte, 1), 1, 254)
    scaled = (w * np.exp2(127.0 - byte)[:, None, :]).reshape(k, n).astype(np.float32)
    by_word = np.ascontiguousarray(scaled.reshape(k // 512, 128, 4, n).transpose(0, 1, 3, 2))
    if fmt == "e4m3":
        words = by_word.astype(ml_dtypes.float8_e4m3fn).view(np.uint8)
    else:
        c = by_word.astype(ml_dtypes.float4_e2m1fn).view(np.uint8) & 0xF
        words = (c[..., 0::2] | (c[..., 1::2] << 4)).reshape(k // 512, 128, 2 * n)
    return np.ascontiguousarray(words), np.ascontiguousarray(byte.astype(np.uint8).reshape(k // 512, 16, n))


def unpack_weight(words, scales, fmt):
    g, _, n = scales.shape
    words = np.ascontiguousarray(words).reshape(g, 128, n, -1)
    if fmt == "e4m3":
        vals = words.view(ml_dtypes.float8_e4m3fn).astype(np.float64)
    else:
        nib = np.empty((g, 128, n, 4), np.uint8)
        nib[..., 0::2] = words & 0xF
        nib[..., 1::2] = words >> 4
        vals = E2M1[nib]
    vals = vals * np.repeat(np.exp2(scales.astype(np.float64) - 127.0), 8, axis=1)[..., None]
    return vals.transpose(0, 1, 3, 2).reshape(g * 512, n)


def sigmoid(v):
    return 1.0 / (1.0 + np.exp(-v))


D, T, Z, I, Q = 512, 1024, 1024, 512, 128


def setup_inputs():
    n = np.random.standard_normal
    idx = np.stack([np.random.permutation(T)[:I] for _ in range(8)])
    idx2 = np.stack([np.random.permutation(Z)[:I] for _ in range(8)])
    idx3 = np.stack([np.random.permutation(Z)[:I] for _ in range(8)])
    fd = mx_kscale(D)
    keysp = pack_weight(n((D, T)) / fd[:, None], "e2m1")
    return {
        "query": (n((D, Q)) * 1.0 / np.sqrt(D) * fd[:, None]).astype(np.float32),
        "keys_words": keysp[0],
        "keys_scales": keysp[1],
        "thr": (np.random.uniform(-0.6, 0.6, (Q, 1))).astype(np.float32),
        "slope": (np.random.uniform(1.0, 3.0, (Q, 1))).astype(np.float32),
        "old": (1.0 * n((Q, Z))).astype(np.float32),
        "offs": striped8(idx),
        "offs2": striped8(idx2),
        "offs3": striped8(idx3),
    }


def reference(query, keys_words, keys_scales, thr, slope, old, offs, offs2, offs3):
    idx = unstriped8(offs)
    idx2 = unstriped8(offs2)
    idx3 = unstriped8(offs3)
    keysu = unpack_weight(keys_words, keys_scales, "e2m1")
    queryq = mxq(f64(query), 0, "e4m3")
    a = queryq.T @ keysu
    s1 = sigmoid(pick8(a, idx, 16) * f64(slope) + f64(thr))
    f1 = np.zeros((Q, Z))
    f1[np.arange(Q)[:, None], idx2[np.arange(Q) % 128 // 16]] = s1
    cc = f64(old) + f1 * 2.0
    tc2 = np.max(cc, axis=1, keepdims=True)
    y = np.exp(pick8(cc, idx3, 16) - tc2)
    return y

@@ -1,0 +1,113 @@
+from contextlib import ExitStack
+
+import concourse.mybir as mybir
+
+D, T, Z, I, Q = 512, 1024, 1024, 512, 128
+FLOPS = 2 * D * T * Q
+
+F32 = mybir.dt.float32
+BF16 = mybir.dt.bfloat16
+I32 = mybir.dt.int32
+U32 = mybir.dt.uint32
+U16 = mybir.dt.uint16
+U8 = mybir.dt.uint8
+FP8X4 = mybir.dt.float8_e4m3fn_x4
+FP4X4 = mybir.dt.float4_e2m1fn_x4
+ALU = mybir.AluOpType
+ACT = mybir.ActivationFunctionType
+AXIS = mybir.AxisListType
+
+P = 128
+PACK = 4
+N_TILE = 256
+HALF = I // 2
+LIST_COLS = HALF // 16
+
+
+def tile_attend_tallied_one_kernel(tc, query, keys_words, keys_scales, thr, slope, old, offs, offs2, offs3, out):
+    nc = tc.nc
+    with ExitStack() as ctx:
+        sb = ctx.enter_context(tc.tile_pool(name="sb", bufs=1))
+        psum = ctx.enter_context(tc.psum_pool(name="psum", bufs=1))
+
+        offs_sb = sb.tile([P, I // 16], U16, name="offs_sb")
+        offs2_sb = sb.tile([P, I // 16], U16, name="offs2_sb")
+        offs3_sb = sb.tile([P, I // 16], U16, name="offs3_sb")
+        q_raw = sb.tile([P, PACK, Q], F32, name="q_raw")
+        k_words = sb.tile([P, 2 * T], U8, name="k_words", align_bytes=64)
+        k_scales = sb.tile([P, T], U8, name="k_scales", align_bytes=64)
+        thr_sb = sb.tile([P, 1], F32, name="thr_sb")
+        slope_sb = sb.tile([P, 1], F32, name="slope_sb")
+        old_sb = sb.tile([P, Z], F32, name="old_sb")
+        gates = sb.tile([P, Z], F32, name="gates")
+
+        nc.vector.memset(k_scales[:].bitcast(I32), 0)
+        nc.vector.memset(gates[:], 0.0)
+
+        nc.sync.dma_start(out=q_raw[:], in_=query.rearrange("(p j) q -> p j q", j=PACK))
+        nc.sync.dma_start(out=k_words[:].bitcast(I32), in_=keys_words[0].bitcast(I32))
+        for quad in range(4):
+            nc.sync.dma_start(
+                out=k_scales[32 * quad : 32 * quad + 4, :].bitcast(I32),
+                in_=keys_scales[0, 4 * quad : 4 * quad + 4, :].bitcast(I32),
+            )
+        nc.gpsimd.dma_start(out=thr_sb[:], in_=thr)
+        nc.sync.dma_start(offs_sb[:], offs)
+        nc.sync.dma_start(out=slope_sb[:], in_=slope)
+        nc.sync.dma_start(offs2_sb[:], offs2)
+        nc.sync.dma_start(out=old_sb[:], in_=old)
+        nc.sync.dma_start(offs3_sb[:], offs3)
+
+        q_grouped = sb.tile([P, Q, PACK], BF16, name="q_grouped", align_bytes=64)
+        q_codes = sb.tile([P, Q], U32, name="q_codes", align_bytes=64)
+        q_scales = sb.tile([P, Q], U8, name="q_scales", align_bytes=64)
+        q_halves = (slice(0, Q // 2), slice(Q // 2, Q))
+        for rows in q_halves:
+            nc.vector.tensor_copy(out=q_grouped[:, rows, :], in_=q_raw[:, :, rows].rearrange("p j q -> p q j"))
+        for rows in q_halves:
+            nc.vector.quantize_mx(
+                out=q_codes[:, rows].bitcast(FP8X4),
+                scales=q_scales[:, rows],
+                in_=q_grouped[:, rows, :].rearrange("p q j -> p (q j)"),
+            )
+
+        scores = sb.tile([P, T], F32, name="scores")
+        for n0 in range(0, T, N_TILE):
+            acc = psum.tile([P, N_TILE], F32, name="acc%d" % (n0 // N_TILE))
+            nc.tensor.matmul_mx(
+                out=acc[:],
+                lhsT=q_codes[:].bitcast(FP8X4),
+                lhsT_scale=q_scales[:],
+                rhs=k_words[:, 2 * n0 : 2 * (n0 + N_TILE)].bitcast(FP4X4),
+                rhs_scale=k_scales[:, n0 : n0 + N_TILE],
+                start=True,
+                stop=True,
+            )
+            nc.vector.tensor_copy(out=scores[:, n0 : n0 + N_TILE], in_=acc[:])
+
+        for h in range(2):
+            cols = slice(h * LIST_COLS, (h + 1) * LIST_COLS)
+            s1 = sb.tile([P, HALF], F32, name="s1_%d" % h)
+            nc.scalar.activation(
+                out=s1[:],
+                in_=scores[:].indirect(offs_sb[:, cols]),
+                func=ACT.Sigmoid,
+                bias=thr_sb[:],
+                scale=slope_sb[:],
+            )
+            nc.vector.tensor_copy(out=gates[:].indirect(offs2_sb[:, cols]), in_=s1[:])
+
+        tally = sb.tile([P, Z], F32, name="tally")
+        nc.vector.scalar_tensor_tensor(
+            out=tally[:], in0=gates[:], scalar=2.0, in1=old_sb[:], op0=ALU.mult, op1=ALU.add
+        )
+        neg_top = sb.tile([P, 1], F32, name="neg_top")
+        nc.vector.tensor_reduce(out=neg_top[:], in_=tally[:], axis=AXIS.X, op=ALU.max, negate=True)
+
+        for h in range(2):
+            cols = slice(h * LIST_COLS, (h + 1) * LIST_COLS)
+            res = sb.tile([P, HALF], F32, name="res_%d" % h)
+            nc.scalar.activation(
+                out=res[:], in_=tally[:].indirect(offs3_sb[:, cols]), func=ACT.Exp, bias=neg_top[:]
+            )
+            nc.sync.dma_start(out=out[:, h * HALF : (h + 1) * HALF], in_=res[:])

@@ -22,6 +22,7 @@ PACK = 4
 N_TILE = 256
 HALF = I // 2
 LIST_COLS = HALF // 16
+FIRST = 128
 
 
 def tile_attend_tallied_one_kernel(tc, query, keys_words, keys_scales, thr, slope, old, offs, offs2, offs3, out):
@@ -43,6 +44,10 @@ def tile_attend_tallied_one_kernel(tc, query, keys_words, keys_scales, thr, slop
 
         nc.vector.memset(k_scales[:].bitcast(I32), 0)
         nc.vector.memset(gates[:], 0.0)
+        gates_b = sb.tile([P, Z], F32, name="gates_b")
+        nc.vector.memset(gates_b[:], 0.0)
+        twos = sb.tile([P, FIRST], F32, name="twos")
+        nc.vector.memset(twos[:], 2.0)
 
         nc.sync.dma_start(out=q_raw[:], in_=query.rearrange("(p j) q -> p j q", j=PACK))
         nc.sync.dma_start(out=k_words[:].bitcast(I32), in_=keys_words[0].bitcast(I32))
@@ -85,21 +90,25 @@ def tile_attend_tallied_one_kernel(tc, query, keys_words, keys_scales, thr, slop
             )
             nc.vector.tensor_copy(out=scores[:, n0 : n0 + N_TILE], in_=acc[:])
 
+        s1 = sb.tile([P, I], F32, name="s1")
         for h in range(2):
             cols = slice(h * LIST_COLS, (h + 1) * LIST_COLS)
-            s1 = sb.tile([P, HALF], F32, name="s1_%d" % h)
             nc.scalar.activation(
-                out=s1[:],
+                out=s1[:, h * HALF : (h + 1) * HALF],
                 in_=scores[:].indirect(offs_sb[:, cols]),
                 func=ACT.Sigmoid,
                 bias=thr_sb[:],
                 scale=slope_sb[:],
             )
-            nc.vector.tensor_copy(out=gates[:].indirect(offs2_sb[:, cols]), in_=s1[:])
-
+        nc.vector.tensor_tensor(
+            out=gates[:].indirect(offs2_sb[:, 0 : FIRST // 16]), in0=s1[:, 0:FIRST], in1=twos[:], op=ALU.mult
+        )
+        nc.vector.tensor_copy(out=gates_b[:].indirect(offs2_sb[:, FIRST // 16 : I // 16]), in_=s1[:, FIRST:I])
+        part = sb.tile([P, Z], F32, name="part")
+        nc.gpsimd.tensor_tensor(out=part[:], in0=gates[:], in1=old_sb[:], op=ALU.add)
         tally = sb.tile([P, Z], F32, name="tally")
         nc.vector.scalar_tensor_tensor(
-            out=tally[:], in0=gates[:], scalar=2.0, in1=old_sb[:], op0=ALU.mult, op1=ALU.add
+            out=tally[:], in0=gates_b[:], scalar=2.0, in1=part[:], op0=ALU.mult, op1=ALU.add
         )
         neg_top = sb.tile([P, 1], F32, name="neg_top")
         nc.vector.tensor_reduce(out=neg_top[:], in_=tally[:], axis=AXIS.X, op=ALU.max, negate=True)

from contextlib import ExitStack

import concourse.mybir as mybir

D, T, Z, I, Q = 512, 1024, 1024, 512, 128
FLOPS = 2 * D * T * Q

F32 = mybir.dt.float32
BF16 = mybir.dt.bfloat16
I32 = mybir.dt.int32
U32 = mybir.dt.uint32
U16 = mybir.dt.uint16
U8 = mybir.dt.uint8
FP8X4 = mybir.dt.float8_e4m3fn_x4
FP4X4 = mybir.dt.float4_e2m1fn_x4
ALU = mybir.AluOpType
ACT = mybir.ActivationFunctionType
AXIS = mybir.AxisListType

P = 128
PACK = 4
N_TILE = 256
HALF = I // 2
LIST_COLS = HALF // 16
FIRST = 128


def tile_attend_tallied_one_kernel(tc, query, keys_words, keys_scales, thr, slope, old, offs, offs2, offs3, out):
    nc = tc.nc
    with ExitStack() as ctx:
        sb = ctx.enter_context(tc.tile_pool(name="sb", bufs=1))
        psum = ctx.enter_context(tc.psum_pool(name="psum", bufs=1))

        offs_sb = sb.tile([P, I // 16], U16, name="offs_sb")
        offs2_sb = sb.tile([P, I // 16], U16, name="offs2_sb")
        offs3_sb = sb.tile([P, I // 16], U16, name="offs3_sb")
        q_raw = sb.tile([P, PACK, Q], F32, name="q_raw")
        k_words = sb.tile([P, 2 * T], U8, name="k_words", align_bytes=64)
        k_scales = sb.tile([P, T], U8, name="k_scales", align_bytes=64)
        thr_sb = sb.tile([P, 1], F32, name="thr_sb")
        slope_sb = sb.tile([P, 1], F32, name="slope_sb")
        old_sb = sb.tile([P, Z], F32, name="old_sb")
        gates = sb.tile([P, Z], F32, name="gates")

        nc.vector.memset(k_scales[:].bitcast(I32), 0)
        nc.vector.memset(gates[:], 0.0)
        gates_b = sb.tile([P, Z], F32, name="gates_b")
        nc.vector.memset(gates_b[:], 0.0)
        twos = sb.tile([P, FIRST], F32, name="twos")
        nc.vector.memset(twos[:], 2.0)

        nc.sync.dma_start(out=q_raw[:], in_=query.rearrange("(p j) q -> p j q", j=PACK))
        nc.sync.dma_start(out=k_words[:].bitcast(I32), in_=keys_words[0].bitcast(I32))
        for quad in range(4):
            nc.sync.dma_start(
                out=k_scales[32 * quad : 32 * quad + 4, :].bitcast(I32),
                in_=keys_scales[0, 4 * quad : 4 * quad + 4, :].bitcast(I32),
            )
        nc.gpsimd.dma_start(out=thr_sb[:], in_=thr)
        nc.sync.dma_start(offs_sb[:], offs)
        nc.sync.dma_start(out=slope_sb[:], in_=slope)
        nc.sync.dma_start(offs2_sb[:], offs2)
        nc.sync.dma_start(out=old_sb[:], in_=old)
        nc.sync.dma_start(offs3_sb[:], offs3)

        q_grouped = sb.tile([P, Q, PACK], BF16, name="q_grouped", align_bytes=64)
        q_codes = sb.tile([P, Q], U32, name="q_codes", align_bytes=64)
        q_scales = sb.tile([P, Q], U8, name="q_scales", align_bytes=64)
        q_halves = (slice(0, Q // 2), slice(Q // 2, Q))
        for rows in q_halves:
            nc.vector.tensor_copy(out=q_grouped[:, rows, :], in_=q_raw[:, :, rows].rearrange("p j q -> p q j"))
        for rows in q_halves:
            nc.vector.quantize_mx(
                out=q_codes[:, rows].bitcast(FP8X4),
                scales=q_scales[:, rows],
                in_=q_grouped[:, rows, :].rearrange("p q j -> p (q j)"),
            )

        scores = sb.tile([P, T], F32, name="scores")
        for n0 in range(0, T, N_TILE):
            acc = psum.tile([P, N_TILE], F32, name="acc%d" % (n0 // N_TILE))
            nc.tensor.matmul_mx(
                out=acc[:],
                lhsT=q_codes[:].bitcast(FP8X4),
                lhsT_scale=q_scales[:],
                rhs=k_words[:, 2 * n0 : 2 * (n0 + N_TILE)].bitcast(FP4X4),
                rhs_scale=k_scales[:, n0 : n0 + N_TILE],
                start=True,
                stop=True,
            )
            nc.vector.tensor_copy(out=scores[:, n0 : n0 + N_TILE], in_=acc[:])

        s1 = sb.tile([P, I], F32, name="s1")
        for h in range(2):
            cols = slice(h * LIST_COLS, (h + 1) * LIST_COLS)
            nc.scalar.activation(
                out=s1[:, h * HALF : (h + 1) * HALF],
                in_=scores[:].indirect(offs_sb[:, cols]),
                func=ACT.Sigmoid,
                bias=thr_sb[:],
                scale=slope_sb[:],
            )
        nc.vector.tensor_tensor(
            out=gates[:].indirect(offs2_sb[:, 0 : FIRST // 16]), in0=s1[:, 0:FIRST], in1=twos[:], op=ALU.mult
        )
        nc.vector.tensor_copy(out=gates_b[:].indirect(offs2_sb[:, FIRST // 16 : I // 16]), in_=s1[:, FIRST:I])
        part = sb.tile([P, Z], F32, name="part")
        nc.gpsimd.tensor_tensor(out=part[:], in0=gates[:], in1=old_sb[:], op=ALU.add)
        tally = sb.tile([P, Z], F32, name="tally")
        nc.vector.scalar_tensor_tensor(
            out=tally[:], in0=gates_b[:], scalar=2.0, in1=part[:], op0=ALU.mult, op1=ALU.add
        )
        neg_top = sb.tile([P, 1], F32, name="neg_top")
        nc.vector.tensor_reduce(out=neg_top[:], in_=tally[:], axis=AXIS.X, op=ALU.max, negate=True)

        for h in range(2):
            cols = slice(h * LIST_COLS, (h + 1) * LIST_COLS)
            res = sb.tile([P, HALF], F32, name="res_%d" % h)
            nc.scalar.activation(
                out=res[:], in_=tally[:].indirect(offs3_sb[:, cols]), func=ACT.Exp, bias=neg_top[:]
            )
            nc.sync.dma_start(out=out[:, h * HALF : (h + 1) * HALF], in_=res[:])
